import numpy as np
CORES = [52,68,84,180,196,212,308,324,340]
N = 9
W = 256
def setup_inputs(rng):
    amp = 0.5 + 1.5 * rng.random((2, N, 128, 1), dtype=np.float32)
    return {"u": amp[0] * rng.standard_normal((N, 128, W), dtype=np.float32), "b": amp[1] * rng.standard_normal((N, 128, W), dtype=np.float32)}
def setup_inputs_big(rng):
    d = setup_inputs(rng)
    for k in ("u", "b"): d[k] = (d[k].astype(np.float32) * 1024.0).astype(d[k].dtype)
    return d
def setup_inputs_small(rng):
    d = setup_inputs(rng)
    for k in ("u", "b"): d[k] = (d[k].astype(np.float32) * (1 / 1024.0)).astype(d[k].dtype)
    return d
def setup_inputs_apart(rng):
    d = setup_inputs(rng)
    f = (10.0 ** rng.permutation(np.linspace(-1.5, 1.5, N))).astype(np.float32).reshape(N, 1, 1)
    for k in ("u", "b"): d[k] = (d[k].astype(np.float32) * f).astype(d[k].dtype)
    return d
def reference(u, b):
    g = np.concatenate(list(u.astype(np.float64)), axis=1); bb = np.concatenate(list(b.astype(np.float64)), axis=1)
    p = np.concatenate([g[:, -2:], g, g[:, :2]], axis=1)
    n = 0.125 * (p[:, :-4] + p[:, 1:-3] + p[:, 3:-1] + p[:, 4:]) + 0.5 * bb
    d = n - g
    s = np.stack([(d ** 2).mean(axis=1), np.abs(d).max(axis=1)], axis=1)
    return {"y": np.stack([n[:, W * r:W * r + W] for r in range(N)]).astype(np.float32), "s": np.broadcast_to(s.astype(np.float32), (N, 128, 2))}

@@ -1,0 +1,261 @@
+from concourse.bass import DstId, RemoteDMATransfer
+from concourse.mybir import AluOpType
+
+N = 9
+W = 256
+LO, HI = 2, W - 2
+F32 = "float32"
+
+SCRATCH = {
+    "U": ("sbuf", [128, W], F32), "B": ("sbuf", [128, W], F32),
+    "F": ("sbuf", [128, N + 2, 12], F32),
+    "c8": ("sbuf", [128, W], F32), "cneg": ("sbuf", [128, W], F32), "chP": ("psum", [128, W], F32),
+    "pS": ("sbuf", [128, W], F32), "vP": ("psum", [128, W], F32), "v8P": ("psum", [128, W], F32),
+    "hbP": ("psum", [128, W], F32), "eS": ("sbuf", [128, W], F32),
+    "dP": ("psum", [128, W], F32), "ndS": ("sbuf", [128, W], F32), "NS": ("sbuf", [128, W], F32),
+    "aL": ("psum", [128, 192], F32), "aR": ("sbuf", [128, 128], F32),
+    "sL": ("psum", [128, 192], F32), "sR": ("sbuf", [128, 128], F32),
+    "a1b": ("sbuf", [128, 64], F32), "s1b": ("sbuf", [128, 64], F32),
+    "TA": ("sbuf", [128, 128], F32), "TS": ("sbuf", [128, 128], F32),
+    "V": ("sbuf", [128, N + 1, 2], F32),
+    "C": ("sbuf", [128, 16, 2], F32),
+    "X": ("sbuf", [128, N + 1, 8], F32), "H": ("sbuf", [128, N + 1, 4], F32),
+    "chb": ("sbuf", [128, N + 1, 2], F32), "c8b": ("sbuf", [128, N + 1, 4], F32), "cnb": ("sbuf", [128, N + 1, 4], F32),
+    "pb": ("sbuf", [128, N + 1, 7], F32), "vb": ("sbuf", [128, N + 1, 4], F32), "v8b": ("sbuf", [128, N + 1, 4], F32),
+    "NB": ("sbuf", [128, N + 1, 4], F32), "eb": ("sbuf", [128, N + 1, 4], F32), "db": ("sbuf", [128, N + 1, 4], F32),
+    "ndb": ("sbuf", [128, N + 1, 4], F32),
+    "ab": ("sbuf", [128, N, 4], F32), "sb": ("sbuf", [128, N, 4], F32),
+    "ab2": ("sbuf", [128, N, 2], F32), "sb2": ("sbuf", [128, N, 2], F32),
+    "FA": ("sbuf", [128, 16], F32), "FS": ("sbuf", [128, 16], F32), "cs": ("sbuf", [128, 4], F32),
+    "S": ("sbuf", [128, 2], F32),
+    "YB": ("sbuf", [128, 2, 4], F32),
+    "SL": ("sbuf", [128, 2], F32),
+}
+SEMAPHORES = ["ul", "bl", "el", "vs", "pready", "nready", "nbready", "sready",
+              "earr", "parr", "yarr", "farr", "lsem", "yst", "sst"]
+
+
+def _bits(m):
+    return [1 << i for i in range(16) if (m >> i) & 1]
+
+
+def rank_program(g, core, T, topo):
+    rank = T.rank_of(core)
+    if rank is None:
+        return
+    cores = list(T.cores)
+    sem = T.sem
+    V = g.vector
+    add, sub, mul, mx = AluOpType.add, AluOpType.subtract, AluOpType.mult, AluOpType.max
+
+    def both(a, b):
+        return topo.may_write(cores[a], cores[b]) and topo.may_write(cores[b], cores[a])
+
+    hubs = [r for r in range(N) if all(both(r, x) for x in range(N) if x != r)]
+    serve = {}
+    for i, k in enumerate([r for r in range(N) if r not in hubs]):
+        same = [h for h in hubs if topo.chip(cores[h]) == topo.chip(cores[k])]
+        serve[k] = same[0] if same else hubs[i % len(hubs)]
+    is_hub = rank in hubs
+    clients = [k for k in range(N) if serve.get(k) == rank]
+
+    def hub_dests(x):
+        return [h for h in hubs if h != x]
+
+    def mask_to(x, dests):
+        m = topo.mask(cores[x], cores[dests[0]])
+        for d_ in dests[1:]:
+            m &= topo.mask(cores[x], cores[d_])
+        return m
+
+    def did(dst):
+        rid, pid = topo.addr(cores[dst], core)
+        return DstId(rid=rid, pnc=pid)
+
+    E = T.F[:, rank + 1, :]
+    g.sync.dma_start(T.U[:], T.u[:]).then_inc(sem.ul, 16)
+    g.scalar.dma_start(T.B[:], T.b[:]).then_inc(sem.bl, 16)
+    g.sync.dma_start(T.F[:, rank + 1, 0:4], T.u[:, 0:4]).then_inc(sem.el, 16)
+    g.scalar.dma_start(T.F[:, rank + 1, 8:10], T.b[:, 0:2]).then_inc(sem.el, 16)
+    g.sync.dma_start(T.F[:, rank + 1, 4:8], T.u[:, W - 4:W]).then_inc(sem.el, 16)
+    g.scalar.dma_start(T.F[:, rank + 1, 10:12], T.b[:, W - 2:W]).then_inc(sem.el, 16)
+
+    sent = 0
+    dests = hub_dests(rank)
+    m_hub = mask_to(rank, dests)
+    g.wait_ge(sem.el, 64)
+    g.remote_dma_fused([RemoteDMATransfer(dst_ids=[did(h) for h in dests], dma_engine_mask=m_hub, remote_sem=sem.earr,
+                                          srcs=[E], dsts=[E for h in dests])], local_sem=sem.lsem)
+    sent += len(_bits(m_hub))
+    g.wait_ge(sem.pready, 2)
+    g.remote_dma_fused([RemoteDMATransfer(dst_ids=[did(h) for h in dests], dma_engine_mask=m_hub, remote_sem=sem.parr,
+                                          srcs=[T.V[:, 0, :]],
+                                          dsts=[T.C[:, rank if rank < h else rank - 1, :] for h in dests])],
+                       local_sem=sem.lsem)
+    sent += len(_bits(m_hub))
+    yb_eng = {}
+    for h in hubs:
+        cl = [k for k in range(N) if serve.get(k) == h]
+        if cl:
+            bits = _bits(mask_to(h, cl))
+            per = 1
+            while per * 2 * len(cl) <= len(bits):
+                per *= 2
+            for i, k in enumerate(cl):
+                yb_eng[k] = sum(bits[i * per:(i + 1) * per])
+    if is_hub and clients:
+        g.wait_ge(sem.nbready, 1)
+        g.remote_dma_fused([RemoteDMATransfer(dst_ids=[did(k)], dma_engine_mask=yb_eng[k], remote_sem=sem.yarr,
+                                              srcs=[T.NB[:, k:k + 2, :]], dsts=[T.YB[:]]) for k in clients],
+                           local_sem=sem.lsem)
+        sent += sum(len(_bits(yb_eng[k])) for k in clients)
+        m_cl = mask_to(rank, clients)
+        g.wait_ge(sem.sready, 2)
+        g.remote_dma_fused([RemoteDMATransfer(dst_ids=[did(k) for k in clients], dma_engine_mask=m_cl,
+                                              remote_sem=sem.farr, srcs=[T.S[:]], dsts=[T.SL[:] for k in clients])],
+                           local_sem=sem.lsem)
+        sent += len(_bits(m_cl))
+    g.wait_ge(sem.lsem, sent)
+
+    st = {"n": 0, "w": 0}
+
+    def vw():
+        if st["w"] < st["n"]:
+            V.wait_ge(sem.vs, st["n"])
+            st["w"] = st["n"]
+
+    def vo(ins):
+        ins.then_inc(sem.vs, 1)
+        st["n"] += 1
+
+    def tt(out, a, b, op):
+        vo(V.tensor_tensor(out, a, b, op))
+
+    vo(V.memset(T.c8[:], 0.125))
+    vo(V.memset(T.chP[:], 0.5))
+    vo(V.memset(T.cneg[:], -1.0))
+    for buf in (T.dP, T.ndS):
+        vo(V.memset(buf[:, 0:LO], 0.0))
+        vo(V.memset(buf[:, HI:W], 0.0))
+    if is_hub:
+        vo(V.memset(T.chb[:], 0.5))
+        vo(V.memset(T.c8b[:], 0.125))
+        vo(V.memset(T.cnb[:], -1.0))
+        vo(V.memset(T.C[:, 13:16, :], 0.0))
+        vo(V.memset(T.cs[:], -1.0 / (N * W)))
+
+    V.wait_ge(sem.ul, 16)
+    tt(T.pS[:, 0:W - 1], T.U[:, 0:W - 1], T.U[:, 1:W], add)
+    vw()
+    tt(T.vP[:, LO:HI], T.pS[:, 0:HI - LO], T.pS[:, 3:W - 1], add)
+    V.wait_ge(sem.bl, 16)
+    tt(T.hbP[:, LO:HI], T.B[:, LO:HI], T.chP[:, LO:HI], mul)
+    vw()
+    tt(T.v8P[:, LO:HI], T.vP[:, LO:HI], T.c8[:, LO:HI], mul)
+    tt(T.eS[:, LO:HI], T.hbP[:, LO:HI], T.U[:, LO:HI], sub)
+    vw()
+    tt(T.dP[:, LO:HI], T.v8P[:, LO:HI], T.eS[:, LO:HI], add)
+    vw()
+    tt(T.ndS[:, LO:HI], T.dP[:, LO:HI], T.cneg[:, LO:HI], mul)
+    vw()
+    tt(T.aL[:, 0:128], T.dP[:, 0:128], T.ndS[:, 0:128], mx)
+    tt(T.aR[:], T.dP[:, 128:256], T.ndS[:, 128:256], mx)
+    tt(T.sL[:, 0:128], T.dP[:, 0:128], T.ndS[:, 0:128], mul)
+    tt(T.sR[:], T.dP[:, 128:256], T.ndS[:, 128:256], mul)
+    vw()
+    tt(T.aL[:, 128:192], T.aL[:, 0:64], T.aR[:, 0:64], mx)
+    tt(T.a1b[:], T.aL[:, 64:128], T.aR[:, 64:128], mx)
+    tt(T.sL[:, 128:192], T.sL[:, 0:64], T.sR[:, 0:64], add)
+    tt(T.s1b[:], T.sL[:, 64:128], T.sR[:, 64:128], add)
+    vw()
+    tt(T.TA[:, 0:64], T.aL[:, 128:192], T.a1b[:], mx)
+    tt(T.TS[:, 0:64], T.sL[:, 128:192], T.s1b[:], add)
+    off, w = 0, 64
+    while w > 2:
+        h = w // 2
+        vw()
+        tt(T.TA[:, off + w:off + w + h], T.TA[:, off:off + h], T.TA[:, off + h:off + w], mx)
+        tt(T.TS[:, off + w:off + w + h], T.TS[:, off:off + h], T.TS[:, off + h:off + w], add)
+        off, w = off + w, h
+    vw()
+    V.tensor_tensor(T.V[:, 0, 1:2], T.TA[:, off:off + 1], T.TA[:, off + 1:off + 2], mx).then_inc(sem.pready, 1)
+    V.tensor_tensor(T.V[:, 0, 0:1], T.TS[:, off:off + 1], T.TS[:, off + 1:off + 2], add).then_inc(sem.pready, 1)
+
+    def new_inner():
+        V.tensor_tensor(T.NS[:, LO:HI], T.dP[:, LO:HI], T.U[:, LO:HI], add).then_inc(sem.nready, 1)
+
+    if not is_hub:
+        new_inner()
+    else:
+        M = N + 1
+        V.wait_ge(sem.el, 64)
+        V.wait_ge(sem.earr, sum(len(_bits(mask_to(x, hub_dests(x)))) for x in range(N) if x != rank))
+        vo(V.tensor_copy(T.F[:, 0, :], T.F[:, N, :]))
+        vo(V.tensor_copy(T.F[:, N + 1, :], T.F[:, 1, :]))
+        vw()
+        vo(V.tensor_copy(T.X[:, :, 0:4], T.F[:, 0:M, 4:8]))
+        vo(V.tensor_copy(T.X[:, :, 4:8], T.F[:, 1:M + 1, 0:4]))
+        tt(T.H[:, :, 0:2], T.F[:, 0:M, 10:12], T.chb[:], mul)
+        tt(T.H[:, :, 2:4], T.F[:, 1:M + 1, 8:10], T.chb[:], mul)
+        vw()
+        tt(T.pb[:], T.X[:, :, 0:7], T.X[:, :, 1:8], add)
+        tt(T.eb[:], T.H[:], T.X[:, :, 2:6], sub)
+        vw()
+        tt(T.vb[:], T.pb[:, :, 0:4], T.pb[:, :, 3:7], add)
+        vw()
+        tt(T.v8b[:], T.vb[:], T.c8b[:], mul)
+        vw()
+        V.tensor_tensor(T.NB[:], T.v8b[:], T.H[:], add).then_inc(sem.nbready, 1)
+        tt(T.db[:], T.v8b[:], T.eb[:], add)
+        vw()
+        tt(T.ndb[:], T.db[:], T.cnb[:], mul)
+        vw()
+        tt(T.ab[:], T.db[:, 0:N, :], T.ndb[:, 0:N, :], mx)
+        tt(T.sb[:], T.db[:, 0:N, :], T.ndb[:, 0:N, :], mul)
+        vw()
+        tt(T.ab2[:], T.ab[:, :, 0:2], T.ab[:, :, 2:4], mx)
+        tt(T.sb2[:], T.sb[:, :, 0:2], T.sb[:, :, 2:4], add)
+        vw()
+        tt(T.V[:, 1:M, 1], T.ab2[:, :, 0], T.ab2[:, :, 1], mx)
+        tt(T.V[:, 1:M, 0], T.sb2[:, :, 0], T.sb2[:, :, 1], add)
+        vw()
+        V.wait_ge(sem.pready, 2)
+        tt(T.C[:, 8:13, 1], T.V[:, 0:5, 1], T.V[:, 5:10, 1], mx)
+        tt(T.C[:, 8:13, 0], T.V[:, 0:5, 0], T.V[:, 5:10, 0], add)
+        vw()
+        V.wait_ge(sem.parr, sum(len(_bits(mask_to(x, hub_dests(x)))) for x in range(N) if x != rank))
+        tt(T.FS[:, 0:8], T.C[:, 0:8, 0], T.C[:, 8:16, 0], add)
+        tt(T.FA[:, 0:8], T.C[:, 0:8, 1], T.C[:, 8:16, 1], mx)
+        vw()
+        tt(T.FS[:, 8:12], T.FS[:, 0:4], T.FS[:, 4:8], add)
+        tt(T.FA[:, 8:12], T.FA[:, 0:4], T.FA[:, 4:8], mx)
+        vw()
+        tt(T.FS[:, 12:14], T.FS[:, 8:10], T.FS[:, 10:12], add)
+        tt(T.FA[:, 12:14], T.FA[:, 8:10], T.FA[:, 10:12], mx)
+        vw()
+        tt(T.FS[:, 14:15], T.FS[:, 12:13], T.FS[:, 13:14], add)
+        V.tensor_tensor(T.S[:, 1:2], T.FA[:, 12:13], T.FA[:, 13:14], mx).then_inc(sem.sready, 1)
+        vw()
+        V.tensor_tensor(T.S[:, 0:1], T.FS[:, 14:15], T.cs[:, 0:1], mul).then_inc(sem.sready, 1)
+        new_inner()
+    vw()
+
+    if is_hub:
+        g.scalar.wait_ge(sem.nbready, 1)
+        g.scalar.dma_start(T.y[:, 0:LO], T.NB[:, rank, 2:4]).then_inc(sem.yst, 16)
+        g.scalar.dma_start(T.y[:, HI:W], T.NB[:, rank + 1, 0:2]).then_inc(sem.yst, 16)
+        g.scalar.wait_ge(sem.nready, 1)
+        g.scalar.dma_start(T.y[:, LO:HI], T.NS[:, LO:HI]).then_inc(sem.yst, 16)
+        g.sync.wait_ge(sem.sready, 2)
+        g.sync.dma_start(T.s[:], T.S[:]).then_inc(sem.sst, 16)
+    else:
+        g.scalar.wait_ge(sem.nready, 1)
+        g.scalar.dma_start(T.y[:, LO:HI], T.NS[:, LO:HI]).then_inc(sem.yst, 16)
+        g.scalar.wait_ge(sem.yarr, len(_bits(yb_eng[rank])))
+        g.scalar.dma_start(T.y[:, 0:LO], T.YB[:, 0, 2:4]).then_inc(sem.yst, 16)
+        g.scalar.dma_start(T.y[:, HI:W], T.YB[:, 1, 0:2]).then_inc(sem.yst, 16)
+        hub = serve[rank]
+        g.sync.wait_ge(sem.farr, len(_bits(mask_to(hub, [k for k in range(N) if serve.get(k) == hub]))))
+        g.sync.dma_start(T.s[:], T.SL[:]).then_inc(sem.sst, 16)
+    g.scalar.wait_ge(sem.yst, 48)
+    g.sync.wait_ge(sem.sst, 16)

@@ -4,17 +4,19 @@ from concourse.mybir import AluOpType
 N = 9
 W = 256
 LO, HI = 2, W - 2
+NG = 4
+GW = W // NG
 F32 = "float32"
 
 SCRATCH = {
     "U": ("sbuf", [128, W], F32), "B": ("sbuf", [128, W], F32),
     "F": ("sbuf", [128, N + 2, 12], F32),
-    "c8": ("sbuf", [128, W], F32), "cneg": ("sbuf", [128, W], F32), "chP": ("psum", [128, W], F32),
-    "pS": ("sbuf", [128, W], F32), "vP": ("psum", [128, W], F32), "v8P": ("psum", [128, W], F32),
-    "hbP": ("psum", [128, W], F32), "eS": ("sbuf", [128, W], F32),
+    "c8": ("sbuf", [128, W], F32), "c4P": ("psum", [128, W], F32),
+    "pS": ("sbuf", [128, NG, GW + 8], F32),
+    "accA": ("psum", [128, W], F32), "accB": ("psum", [128, W], F32), "nP": ("psum", [128, W], F32),
     "dP": ("psum", [128, W], F32), "ndS": ("sbuf", [128, W], F32), "NS": ("sbuf", [128, W], F32),
-    "aL": ("psum", [128, 192], F32), "aR": ("sbuf", [128, 128], F32),
-    "sL": ("psum", [128, 192], F32), "sR": ("sbuf", [128, 128], F32),
+    "aP": ("psum", [128, 192], F32), "aS": ("sbuf", [128, 128], F32),
+    "sP": ("psum", [128, 192], F32), "sS": ("sbuf", [128, 128], F32),
     "a1b": ("sbuf", [128, 64], F32), "s1b": ("sbuf", [128, 64], F32),
     "TA": ("sbuf", [128, 128], F32), "TS": ("sbuf", [128, 128], F32),
     "V": ("sbuf", [128, N + 1, 2], F32),
@@ -31,7 +33,7 @@ SCRATCH = {
     "YB": ("sbuf", [128, 2, 4], F32),
     "SL": ("sbuf", [128, 2], F32),
 }
-SEMAPHORES = ["ul", "bl", "el", "vs", "pready", "nready", "nbready", "sready",
+SEMAPHORES = ["ul", "bl", "el", "vs", "k0", "k1", "k2", "k3", "pready", "nready", "nbready", "sready",
               "earr", "parr", "yarr", "farr", "lsem", "yst", "sst"]
 
 
@@ -117,23 +119,32 @@ def rank_program(g, core, T, topo):
         sent += len(_bits(m_cl))
     g.wait_ge(sem.lsem, sent)
 
-    st = {"n": 0, "w": 0}
+    ch = {"vs": [0, 0], "k0": [0, 0], "k1": [0, 0], "k2": [0, 0], "k3": [0, 0]}
+
+    def need(*names):
+        for nm in names:
+            if ch[nm][1] < ch[nm][0]:
+                V.wait_ge(sem[nm], ch[nm][0])
+                ch[nm][1] = ch[nm][0]
+
+    def on(nm, ins):
+        ins.then_inc(sem[nm], 1)
+        ch[nm][0] += 1
+
+    def tk(nm, out, a, b, op):
+        on(nm, V.tensor_tensor(out, a, b, op))
 
     def vw():
-        if st["w"] < st["n"]:
-            V.wait_ge(sem.vs, st["n"])
-            st["w"] = st["n"]
+        need("vs")
 
     def vo(ins):
-        ins.then_inc(sem.vs, 1)
-        st["n"] += 1
+        on("vs", ins)
 
     def tt(out, a, b, op):
-        vo(V.tensor_tensor(out, a, b, op))
+        tk("vs", out, a, b, op)
 
+    vo(V.memset(T.c4P[:], 4.0))
     vo(V.memset(T.c8[:], 0.125))
-    vo(V.memset(T.chP[:], 0.5))
-    vo(V.memset(T.cneg[:], -1.0))
     for buf in (T.dP, T.ndS):
         vo(V.memset(buf[:, 0:LO], 0.0))
         vo(V.memset(buf[:, HI:W], 0.0))
@@ -144,45 +155,60 @@ def rank_program(g, core, T, topo):
         vo(V.memset(T.C[:, 13:16, :], 0.0))
         vo(V.memset(T.cs[:], -1.0 / (N * W)))
 
+    G = range(NG)
+    K = ["k%d" % q for q in G]
+    lo = [max(LO, q * GW) for q in G]
+    hi = [min(HI, (q + 1) * GW) for q in G]
     V.wait_ge(sem.ul, 16)
-    tt(T.pS[:, 0:W - 1], T.U[:, 0:W - 1], T.U[:, 1:W], add)
-    vw()
-    tt(T.vP[:, LO:HI], T.pS[:, 0:HI - LO], T.pS[:, 3:W - 1], add)
+    for q in G:
+        tk(K[q], T.pS[:, q, 0:hi[q] - lo[q] + 3], T.U[:, lo[q] - 2:hi[q] + 1], T.U[:, lo[q] - 1:hi[q] + 2], add)
     V.wait_ge(sem.bl, 16)
-    tt(T.hbP[:, LO:HI], T.B[:, LO:HI], T.chP[:, LO:HI], mul)
     vw()
-    tt(T.v8P[:, LO:HI], T.vP[:, LO:HI], T.c8[:, LO:HI], mul)
-    tt(T.eS[:, LO:HI], T.hbP[:, LO:HI], T.U[:, LO:HI], sub)
-    vw()
-    tt(T.dP[:, LO:HI], T.v8P[:, LO:HI], T.eS[:, LO:HI], add)
-    vw()
-    tt(T.ndS[:, LO:HI], T.dP[:, LO:HI], T.cneg[:, LO:HI], mul)
-    vw()
-    tt(T.aL[:, 0:128], T.dP[:, 0:128], T.ndS[:, 0:128], mx)
-    tt(T.aR[:], T.dP[:, 128:256], T.ndS[:, 128:256], mx)
-    tt(T.sL[:, 0:128], T.dP[:, 0:128], T.ndS[:, 0:128], mul)
-    tt(T.sR[:], T.dP[:, 128:256], T.ndS[:, 128:256], mul)
-    vw()
-    tt(T.aL[:, 128:192], T.aL[:, 0:64], T.aR[:, 0:64], mx)
-    tt(T.a1b[:], T.aL[:, 64:128], T.aR[:, 64:128], mx)
-    tt(T.sL[:, 128:192], T.sL[:, 0:64], T.sR[:, 0:64], add)
-    tt(T.s1b[:], T.sL[:, 64:128], T.sR[:, 64:128], add)
-    vw()
-    tt(T.TA[:, 0:64], T.aL[:, 128:192], T.a1b[:], mx)
-    tt(T.TS[:, 0:64], T.sL[:, 128:192], T.s1b[:], add)
+    for q in G:
+        tk(K[q], T.accA[:, lo[q]:hi[q]], T.B[:, lo[q]:hi[q]], T.c4P[:, lo[q]:hi[q]], mul)
+    for q in G:
+        need(K[q])
+        tk(K[q], T.accB[:, lo[q]:hi[q]], T.accA[:, lo[q]:hi[q]], T.pS[:, q, 0:hi[q] - lo[q]], add)
+    for q in G:
+        need(K[q])
+        tk(K[q], T.accA[:, lo[q]:hi[q]], T.accB[:, lo[q]:hi[q]], T.pS[:, q, 3:hi[q] - lo[q] + 3], add)
+    for q in G:
+        need(K[q])
+        tk(K[q], T.nP[:, lo[q]:hi[q]], T.accA[:, lo[q]:hi[q]], T.c8[:, lo[q]:hi[q]], mul)
+    for q in G:
+        need(K[q])
+        tk(K[q], T.dP[:, lo[q]:hi[q]], T.nP[:, lo[q]:hi[q]], T.U[:, lo[q]:hi[q]], sub)
+        tk(K[q], T.ndS[:, lo[q]:hi[q]], T.U[:, lo[q]:hi[q]], T.nP[:, lo[q]:hi[q]], sub)
+    for q in G:
+        need(K[q])
+        c0, c1 = q * GW, (q + 1) * GW
+        o0, o1 = (q // 2) * GW, (q // 2 + 1) * GW
+        tk(K[q], (T.aP if q % 2 == 0 else T.aS)[:, o0:o1], T.dP[:, c0:c1], T.ndS[:, c0:c1], mx)
+        tk(K[q], (T.sP if q % 2 == 0 else T.sS)[:, o0:o1], T.dP[:, c0:c1], T.ndS[:, c0:c1], mul)
+    need("k0", "k1")
+    tk("k0", T.aP[:, 128:192], T.aP[:, 0:64], T.aS[:, 0:64], mx)
+    tk("k0", T.sP[:, 128:192], T.sP[:, 0:64], T.sS[:, 0:64], add)
+    need("k2", "k3")
+    tk("k2", T.a1b[:], T.aP[:, 64:128], T.aS[:, 64:128], mx)
+    tk("k2", T.s1b[:], T.sP[:, 64:128], T.sS[:, 64:128], add)
+    need("k0", "k2")
+    tk("k0", T.TA[:, 0:64], T.aP[:, 128:192], T.a1b[:], mx)
+    tk("k2", T.TS[:, 0:64], T.sP[:, 128:192], T.s1b[:], add)
     off, w = 0, 64
     while w > 2:
         h = w // 2
-        vw()
-        tt(T.TA[:, off + w:off + w + h], T.TA[:, off:off + h], T.TA[:, off + h:off + w], mx)
-        tt(T.TS[:, off + w:off + w + h], T.TS[:, off:off + h], T.TS[:, off + h:off + w], add)
+        need("k0")
+        tk("k0", T.TA[:, off + w:off + w + h], T.TA[:, off:off + h], T.TA[:, off + h:off + w], mx)
+        need("k2")
+        tk("k2", T.TS[:, off + w:off + w + h], T.TS[:, off:off + h], T.TS[:, off + h:off + w], add)
         off, w = off + w, h
-    vw()
+    need("k0")
     V.tensor_tensor(T.V[:, 0, 1:2], T.TA[:, off:off + 1], T.TA[:, off + 1:off + 2], mx).then_inc(sem.pready, 1)
+    need("k2")
     V.tensor_tensor(T.V[:, 0, 0:1], T.TS[:, off:off + 1], T.TS[:, off + 1:off + 2], add).then_inc(sem.pready, 1)
 
     def new_inner():
-        V.tensor_tensor(T.NS[:, LO:HI], T.dP[:, LO:HI], T.U[:, LO:HI], add).then_inc(sem.nready, 1)
+        V.tensor_copy(T.NS[:, LO:HI], T.nP[:, LO:HI]).then_inc(sem.nready, 1)
 
     if not is_hub:
         new_inner()
@@ -238,7 +264,7 @@ def rank_program(g, core, T, topo):
         vw()
         V.tensor_tensor(T.S[:, 0:1], T.FS[:, 14:15], T.cs[:, 0:1], mul).then_inc(sem.sready, 1)
         new_inner()
-    vw()
+    need("vs", "k0", "k1", "k2", "k3")
 
     if is_hub:
         g.scalar.wait_ge(sem.nbready, 1)

@@ -1,40 +1,36 @@
 from concourse.bass import DstId, RemoteDMATransfer
-from concourse.mybir import AluOpType
+from concourse.mybir import AluOpType, AxisListType, ActivationFunctionType
 
 N = 9
 W = 256
 LO, HI = 2, W - 2
 NG = 4
 GW = W // NG
+M = N + 1
+SW = 2 * NG
 F32 = "float32"
 
 SCRATCH = {
     "U": ("sbuf", [128, W], F32), "B": ("sbuf", [128, W], F32),
-    "F": ("sbuf", [128, N + 2, 12], F32),
-    "c8": ("sbuf", [128, W], F32), "c4P": ("psum", [128, W], F32),
+    "F": ("sbuf", [128, N, 12], F32),
     "pS": ("sbuf", [128, NG, GW + 8], F32),
-    "accA": ("psum", [128, W], F32), "accB": ("psum", [128, W], F32), "nP": ("psum", [128, W], F32),
-    "dP": ("psum", [128, W], F32), "ndS": ("sbuf", [128, W], F32), "NS": ("sbuf", [128, W], F32),
-    "aP": ("psum", [128, 192], F32), "aS": ("sbuf", [128, 128], F32),
-    "sP": ("psum", [128, 192], F32), "sS": ("sbuf", [128, 128], F32),
-    "a1b": ("sbuf", [128, 64], F32), "s1b": ("sbuf", [128, 64], F32),
-    "TA": ("sbuf", [128, 128], F32), "TS": ("sbuf", [128, 128], F32),
-    "V": ("sbuf", [128, N + 1, 2], F32),
-    "C": ("sbuf", [128, 16, 2], F32),
-    "X": ("sbuf", [128, N + 1, 8], F32), "H": ("sbuf", [128, N + 1, 4], F32),
-    "chb": ("sbuf", [128, N + 1, 2], F32), "c8b": ("sbuf", [128, N + 1, 4], F32), "cnb": ("sbuf", [128, N + 1, 4], F32),
-    "pb": ("sbuf", [128, N + 1, 7], F32), "vb": ("sbuf", [128, N + 1, 4], F32), "v8b": ("sbuf", [128, N + 1, 4], F32),
-    "NB": ("sbuf", [128, N + 1, 4], F32), "eb": ("sbuf", [128, N + 1, 4], F32), "db": ("sbuf", [128, N + 1, 4], F32),
-    "ndb": ("sbuf", [128, N + 1, 4], F32),
-    "ab": ("sbuf", [128, N, 4], F32), "sb": ("sbuf", [128, N, 4], F32),
-    "ab2": ("sbuf", [128, N, 2], F32), "sb2": ("sbuf", [128, N, 2], F32),
-    "FA": ("sbuf", [128, 16], F32), "FS": ("sbuf", [128, 16], F32), "cs": ("sbuf", [128, 4], F32),
+    "A0": ("psum", [128, 512], F32), "A1": ("psum", [128, 512], F32),
+    "A2": ("psum", [128, 512], F32), "A3": ("psum", [128, 512], F32),
+    "mS": ("sbuf", [128, W], F32), "R3": ("sbuf", [128, W], F32), "J": ("sbuf", [128, W], F32),
+    "NS": ("sbuf", [128, W], F32),
+    "C": ("sbuf", [128, SW * (N + 1)], F32),
+    "X": ("sbuf", [128, M, 8], F32), "H": ("sbuf", [128, M, 4], F32), "M8": ("sbuf", [128, M, 4], F32),
+    "pb": ("sbuf", [128, M, 7], F32), "vb": ("sbuf", [128, M, 4], F32), "eb": ("sbuf", [128, M, 4], F32),
+    "db": ("sbuf", [128, M, 4], F32), "nb": ("sbuf", [128, M, 4], F32), "NB": ("sbuf", [128, M, 4], F32),
+    "jb": ("sbuf", [128, M, 4], F32),
+    "FM": ("sbuf", [128, 4], F32),
     "S": ("sbuf", [128, 2], F32),
     "YB": ("sbuf", [128, 2, 4], F32),
     "SL": ("sbuf", [128, 2], F32),
 }
 SEMAPHORES = ["ul", "bl", "el", "vs", "k0", "k1", "k2", "k3", "pready", "nready", "nbready", "sready",
-              "earr", "parr", "yarr", "farr", "lsem", "yst", "sst"]
+              "xs", "hs", "ps", "es", "ws", "ds", "n8", "cs", "fm",
+              "earr", "parr", "yarr", "farr", "lsem", "yst", "bst", "sst"]
 
 
 def _bits(m):
@@ -48,7 +44,10 @@ def rank_program(g, core, T, topo):
     cores = list(T.cores)
     sem = T.sem
     V = g.vector
-    add, sub, mul, mx = AluOpType.add, AluOpType.subtract, AluOpType.mult, AluOpType.max
+    A = g.scalar
+    add, mul, mx = AluOpType.add, AluOpType.mult, AluOpType.max
+    AX = AxisListType.X
+    Copy, Square = ActivationFunctionType.Copy, ActivationFunctionType.Square
 
     def both(a, b):
         return topo.may_write(cores[a], cores[b]) and topo.may_write(cores[b], cores[a])
@@ -74,13 +73,14 @@ def rank_program(g, core, T, topo):
         rid, pid = topo.addr(cores[dst], core)
         return DstId(rid=rid, pnc=pid)
 
-    E = T.F[:, rank + 1, :]
+    E = T.F[:, rank, :]
+    OWN = T.C[:, SW * rank:SW * rank + SW]
     g.sync.dma_start(T.U[:], T.u[:]).then_inc(sem.ul, 16)
     g.scalar.dma_start(T.B[:], T.b[:]).then_inc(sem.bl, 16)
-    g.sync.dma_start(T.F[:, rank + 1, 0:4], T.u[:, 0:4]).then_inc(sem.el, 16)
-    g.scalar.dma_start(T.F[:, rank + 1, 8:10], T.b[:, 0:2]).then_inc(sem.el, 16)
-    g.sync.dma_start(T.F[:, rank + 1, 4:8], T.u[:, W - 4:W]).then_inc(sem.el, 16)
-    g.scalar.dma_start(T.F[:, rank + 1, 10:12], T.b[:, W - 2:W]).then_inc(sem.el, 16)
+    g.sync.dma_start(T.F[:, rank, 0:4], T.u[:, 0:4]).then_inc(sem.el, 16)
+    g.scalar.dma_start(T.F[:, rank, 8:10], T.b[:, 0:2]).then_inc(sem.el, 16)
+    g.sync.dma_start(T.F[:, rank, 4:8], T.u[:, W - 4:W]).then_inc(sem.el, 16)
+    g.scalar.dma_start(T.F[:, rank, 10:12], T.b[:, W - 2:W]).then_inc(sem.el, 16)
 
     sent = 0
     dests = hub_dests(rank)
@@ -89,11 +89,9 @@ def rank_program(g, core, T, topo):
     g.remote_dma_fused([RemoteDMATransfer(dst_ids=[did(h) for h in dests], dma_engine_mask=m_hub, remote_sem=sem.earr,
                                           srcs=[E], dsts=[E for h in dests])], local_sem=sem.lsem)
     sent += len(_bits(m_hub))
-    g.wait_ge(sem.pready, 2)
+    g.wait_ge(sem.pready, 2 * NG)
     g.remote_dma_fused([RemoteDMATransfer(dst_ids=[did(h) for h in dests], dma_engine_mask=m_hub, remote_sem=sem.parr,
-                                          srcs=[T.V[:, 0, :]],
-                                          dsts=[T.C[:, rank if rank < h else rank - 1, :] for h in dests])],
-                       local_sem=sem.lsem)
+                                          srcs=[OWN], dsts=[OWN for h in dests])], local_sem=sem.lsem)
     sent += len(_bits(m_hub))
     yb_eng = {}
     for h in hubs:
@@ -119,169 +117,111 @@ def rank_program(g, core, T, topo):
         sent += len(_bits(m_cl))
     g.wait_ge(sem.lsem, sent)
 
-    ch = {"vs": [0, 0], "k0": [0, 0], "k1": [0, 0], "k2": [0, 0], "k3": [0, 0]}
-
-    def need(*names):
-        for nm in names:
-            if ch[nm][1] < ch[nm][0]:
-                V.wait_ge(sem[nm], ch[nm][0])
-                ch[nm][1] = ch[nm][0]
-
-    def on(nm, ins):
-        ins.then_inc(sem[nm], 1)
-        ch[nm][0] += 1
-
-    def tk(nm, out, a, b, op):
-        on(nm, V.tensor_tensor(out, a, b, op))
-
-    def vw():
-        need("vs")
-
-    def vo(ins):
-        on("vs", ins)
-
-    def tt(out, a, b, op):
-        tk("vs", out, a, b, op)
-
-    vo(V.memset(T.c4P[:], 4.0))
-    vo(V.memset(T.c8[:], 0.125))
-    for buf in (T.dP, T.ndS):
-        vo(V.memset(buf[:, 0:LO], 0.0))
-        vo(V.memset(buf[:, HI:W], 0.0))
-    if is_hub:
-        vo(V.memset(T.chb[:], 0.5))
-        vo(V.memset(T.c8b[:], 0.125))
-        vo(V.memset(T.cnb[:], -1.0))
-        vo(V.memset(T.C[:, 13:16, :], 0.0))
-        vo(V.memset(T.cs[:], -1.0 / (N * W)))
-
     G = range(NG)
-    K = ["k%d" % q for q in G]
+    K = [sem["k%d" % q] for q in G]
+    AP = [T["A%d" % q] for q in G]
     lo = [max(LO, q * GW) for q in G]
     hi = [min(HI, (q + 1) * GW) for q in G]
+    wd = [hi[q] - lo[q] for q in G]
+    own = SW * rank
+    arrivals = sum(len(_bits(mask_to(x, hub_dests(x)))) for x in range(N) if x != rank)
+
+    if is_hub:
+        V.memset(T.C[:, SW * N + 3:SW * N + SW:2], 0.0).then_inc(sem.vs, 1)
+
+    A.wait_ge(sem.ul, 16)
+    A.wait_ge(sem.bl, 16)
+    for q in G:
+        A.activation(AP[q][:, 0:wd[q]], T.B[:, lo[q]:hi[q]], Copy, scale=4.0).then_inc(K[q], 1)
+        A.activation(T.mS[:, lo[q]:hi[q]], T.U[:, lo[q]:hi[q]], Copy, scale=-8.0).then_inc(K[q], 1)
     V.wait_ge(sem.ul, 16)
     for q in G:
-        tk(K[q], T.pS[:, q, 0:hi[q] - lo[q] + 3], T.U[:, lo[q] - 2:hi[q] + 1], T.U[:, lo[q] - 1:hi[q] + 2], add)
-    V.wait_ge(sem.bl, 16)
-    vw()
+        V.tensor_tensor(T.pS[:, q, 0:wd[q] + 3], T.U[:, lo[q] - 2:hi[q] + 1], T.U[:, lo[q] - 1:hi[q] + 2],
+                        add).then_inc(K[q], 1)
     for q in G:
-        tk(K[q], T.accA[:, lo[q]:hi[q]], T.B[:, lo[q]:hi[q]], T.c4P[:, lo[q]:hi[q]], mul)
+        V.wait_ge(K[q], 3)
+        V.tensor_tensor(AP[q][:, 0:wd[q]], AP[q][:, 0:wd[q]], T.pS[:, q, 0:wd[q]], add).then_inc(K[q], 1)
     for q in G:
-        need(K[q])
-        tk(K[q], T.accB[:, lo[q]:hi[q]], T.accA[:, lo[q]:hi[q]], T.pS[:, q, 0:hi[q] - lo[q]], add)
+        V.wait_ge(K[q], 4)
+        V.tensor_tensor(AP[q][:, 0:wd[q]], AP[q][:, 0:wd[q]], T.pS[:, q, 3:wd[q] + 3], add).then_inc(K[q], 1)
     for q in G:
-        need(K[q])
-        tk(K[q], T.accA[:, lo[q]:hi[q]], T.accB[:, lo[q]:hi[q]], T.pS[:, q, 3:hi[q] - lo[q] + 3], add)
+        V.wait_ge(K[q], 5)
+        V.tensor_tensor(T.R3[:, lo[q]:hi[q]], AP[q][:, 0:wd[q]], T.mS[:, lo[q]:hi[q]], add).then_inc(K[q], 1)
     for q in G:
-        need(K[q])
-        tk(K[q], T.nP[:, lo[q]:hi[q]], T.accA[:, lo[q]:hi[q]], T.c8[:, lo[q]:hi[q]], mul)
+        V.wait_ge(K[q], 6)
+        V.tensor_reduce(T.C[:, own + 2 * q:own + 2 * q + 1], T.R3[:, lo[q]:hi[q]], AX, mx,
+                        apply_absolute_value=True).then_inc(sem.pready, 1)
     for q in G:
-        need(K[q])
-        tk(K[q], T.dP[:, lo[q]:hi[q]], T.nP[:, lo[q]:hi[q]], T.U[:, lo[q]:hi[q]], sub)
-        tk(K[q], T.ndS[:, lo[q]:hi[q]], T.U[:, lo[q]:hi[q]], T.nP[:, lo[q]:hi[q]], sub)
-    for q in G:
-        need(K[q])
-        c0, c1 = q * GW, (q + 1) * GW
-        o0, o1 = (q // 2) * GW, (q // 2 + 1) * GW
-        tk(K[q], (T.aP if q % 2 == 0 else T.aS)[:, o0:o1], T.dP[:, c0:c1], T.ndS[:, c0:c1], mx)
-        tk(K[q], (T.sP if q % 2 == 0 else T.sS)[:, o0:o1], T.dP[:, c0:c1], T.ndS[:, c0:c1], mul)
-    need("k0", "k1")
-    tk("k0", T.aP[:, 128:192], T.aP[:, 0:64], T.aS[:, 0:64], mx)
-    tk("k0", T.sP[:, 128:192], T.sP[:, 0:64], T.sS[:, 0:64], add)
-    need("k2", "k3")
-    tk("k2", T.a1b[:], T.aP[:, 64:128], T.aS[:, 64:128], mx)
-    tk("k2", T.s1b[:], T.sP[:, 64:128], T.sS[:, 64:128], add)
-    need("k0", "k2")
-    tk("k0", T.TA[:, 0:64], T.aP[:, 128:192], T.a1b[:], mx)
-    tk("k2", T.TS[:, 0:64], T.sP[:, 128:192], T.s1b[:], add)
-    off, w = 0, 64
-    while w > 2:
-        h = w // 2
-        need("k0")
-        tk("k0", T.TA[:, off + w:off + w + h], T.TA[:, off:off + h], T.TA[:, off + h:off + w], mx)
-        need("k2")
-        tk("k2", T.TS[:, off + w:off + w + h], T.TS[:, off:off + h], T.TS[:, off + h:off + w], add)
-        off, w = off + w, h
-    need("k0")
-    V.tensor_tensor(T.V[:, 0, 1:2], T.TA[:, off:off + 1], T.TA[:, off + 1:off + 2], mx).then_inc(sem.pready, 1)
-    need("k2")
-    V.tensor_tensor(T.V[:, 0, 0:1], T.TS[:, off:off + 1], T.TS[:, off + 1:off + 2], add).then_inc(sem.pready, 1)
+        A.wait_ge(K[q], 6)
+        A.activation(T.J[:, lo[q]:hi[q]], T.R3[:, lo[q]:hi[q]], Square, scale=1.0 / 384.0,
+                     accum_out=T.C[:, own + 2 * q + 1:own + 2 * q + 2]).then_inc(sem.pready, 1)
 
     def new_inner():
-        V.tensor_copy(T.NS[:, LO:HI], T.nP[:, LO:HI]).then_inc(sem.nready, 1)
+        for q in G:
+            A.activation(T.NS[:, lo[q]:hi[q]], AP[q][:, 0:wd[q]], Copy, scale=0.125).then_inc(sem.nready, 1)
 
     if not is_hub:
         new_inner()
     else:
-        M = N + 1
+        sl = SW * N
         V.wait_ge(sem.el, 64)
-        V.wait_ge(sem.earr, sum(len(_bits(mask_to(x, hub_dests(x)))) for x in range(N) if x != rank))
-        vo(V.tensor_copy(T.F[:, 0, :], T.F[:, N, :]))
-        vo(V.tensor_copy(T.F[:, N + 1, :], T.F[:, 1, :]))
-        vw()
-        vo(V.tensor_copy(T.X[:, :, 0:4], T.F[:, 0:M, 4:8]))
-        vo(V.tensor_copy(T.X[:, :, 4:8], T.F[:, 1:M + 1, 0:4]))
-        tt(T.H[:, :, 0:2], T.F[:, 0:M, 10:12], T.chb[:], mul)
-        tt(T.H[:, :, 2:4], T.F[:, 1:M + 1, 8:10], T.chb[:], mul)
-        vw()
-        tt(T.pb[:], T.X[:, :, 0:7], T.X[:, :, 1:8], add)
-        tt(T.eb[:], T.H[:], T.X[:, :, 2:6], sub)
-        vw()
-        tt(T.vb[:], T.pb[:, :, 0:4], T.pb[:, :, 3:7], add)
-        vw()
-        tt(T.v8b[:], T.vb[:], T.c8b[:], mul)
-        vw()
-        V.tensor_tensor(T.NB[:], T.v8b[:], T.H[:], add).then_inc(sem.nbready, 1)
-        tt(T.db[:], T.v8b[:], T.eb[:], add)
-        vw()
-        tt(T.ndb[:], T.db[:], T.cnb[:], mul)
-        vw()
-        tt(T.ab[:], T.db[:, 0:N, :], T.ndb[:, 0:N, :], mx)
-        tt(T.sb[:], T.db[:, 0:N, :], T.ndb[:, 0:N, :], mul)
-        vw()
-        tt(T.ab2[:], T.ab[:, :, 0:2], T.ab[:, :, 2:4], mx)
-        tt(T.sb2[:], T.sb[:, :, 0:2], T.sb[:, :, 2:4], add)
-        vw()
-        tt(T.V[:, 1:M, 1], T.ab2[:, :, 0], T.ab2[:, :, 1], mx)
-        tt(T.V[:, 1:M, 0], T.sb2[:, :, 0], T.sb2[:, :, 1], add)
-        vw()
-        V.wait_ge(sem.pready, 2)
-        tt(T.C[:, 8:13, 1], T.V[:, 0:5, 1], T.V[:, 5:10, 1], mx)
-        tt(T.C[:, 8:13, 0], T.V[:, 0:5, 0], T.V[:, 5:10, 0], add)
-        vw()
-        V.wait_ge(sem.parr, sum(len(_bits(mask_to(x, hub_dests(x)))) for x in range(N) if x != rank))
-        tt(T.FS[:, 0:8], T.C[:, 0:8, 0], T.C[:, 8:16, 0], add)
-        tt(T.FA[:, 0:8], T.C[:, 0:8, 1], T.C[:, 8:16, 1], mx)
-        vw()
-        tt(T.FS[:, 8:12], T.FS[:, 0:4], T.FS[:, 4:8], add)
-        tt(T.FA[:, 8:12], T.FA[:, 0:4], T.FA[:, 4:8], mx)
-        vw()
-        tt(T.FS[:, 12:14], T.FS[:, 8:10], T.FS[:, 10:12], add)
-        tt(T.FA[:, 12:14], T.FA[:, 8:10], T.FA[:, 10:12], mx)
-        vw()
-        tt(T.FS[:, 14:15], T.FS[:, 12:13], T.FS[:, 13:14], add)
-        V.tensor_tensor(T.S[:, 1:2], T.FA[:, 12:13], T.FA[:, 13:14], mx).then_inc(sem.sready, 1)
-        vw()
-        V.tensor_tensor(T.S[:, 0:1], T.FS[:, 14:15], T.cs[:, 0:1], mul).then_inc(sem.sready, 1)
+        V.wait_ge(sem.earr, arrivals)
+        V.tensor_copy(T.X[:, 1:M, 0:4], T.F[:, 0:N, 4:8]).then_inc(sem.xs, 1)
+        V.tensor_copy(T.X[:, 0:N, 4:8], T.F[:, 0:N, 0:4]).then_inc(sem.xs, 1)
+        V.tensor_copy(T.X[:, 0, 0:4], T.F[:, N - 1, 4:8]).then_inc(sem.xs, 1)
+        V.tensor_copy(T.X[:, N, 4:8], T.F[:, 0, 0:4]).then_inc(sem.xs, 1)
+        A.wait_ge(sem.el, 64)
+        A.wait_ge(sem.earr, arrivals)
+        A.activation(T.H[:, 1:M, 0:2], T.F[:, 0:N, 10:12], Copy, scale=4.0).then_inc(sem.hs, 1)
+        A.activation(T.H[:, 0:N, 2:4], T.F[:, 0:N, 8:10], Copy, scale=4.0).then_inc(sem.hs, 1)
+        A.activation(T.H[:, 0, 0:2], T.F[:, N - 1, 10:12], Copy, scale=4.0).then_inc(sem.hs, 1)
+        A.activation(T.H[:, N, 2:4], T.F[:, 0, 8:10], Copy, scale=4.0).then_inc(sem.hs, 1)
+        A.wait_ge(sem.xs, 4)
+        A.activation(T.M8[:], T.X[:, :, 2:6], Copy, scale=-8.0).then_inc(sem.hs, 1)
+        V.wait_ge(sem.xs, 4)
+        V.tensor_tensor(T.pb[:], T.X[:, :, 0:7], T.X[:, :, 1:8], add).then_inc(sem.ps, 1)
+        V.wait_ge(sem.hs, 5)
+        V.tensor_tensor(T.eb[:], T.H[:], T.M8[:], add).then_inc(sem.es, 1)
+        V.wait_ge(sem.ps, 1)
+        V.tensor_tensor(T.vb[:], T.pb[:, :, 0:4], T.pb[:, :, 3:7], add).then_inc(sem.ws, 1)
+        V.wait_ge(sem.es, 1)
+        V.wait_ge(sem.ws, 1)
+        V.tensor_tensor(T.db[:], T.vb[:], T.eb[:], add).then_inc(sem.ds, 1)
+        V.tensor_tensor(T.nb[:], T.vb[:], T.H[:], add).then_inc(sem.n8, 1)
+        V.wait_ge(sem.ds, 1)
+        for j in range(4):
+            V.tensor_reduce(T.C[:, sl + 2 * j:sl + 2 * j + 1], T.db[:, 0:N, j], AX, mx,
+                            apply_absolute_value=True).then_inc(sem.cs, 1)
+        A.wait_ge(sem.ds, 1)
+        A.activation(T.jb[:, 0:N, :], T.db[:, 0:N, :], Square, scale=1.0 / 384.0,
+                     accum_out=T.C[:, sl + 1:sl + 2]).then_inc(sem.cs, 1)
+        A.wait_ge(sem.n8, 1)
+        A.activation(T.NB[:], T.nb[:], Copy, scale=0.125).then_inc(sem.nbready, 1)
         new_inner()
-    need("vs", "k0", "k1", "k2", "k3")
+        V.wait_ge(sem.vs, 1)
+        V.wait_ge(sem.cs, 5)
+        V.wait_ge(sem.pready, 2 * NG)
+        V.wait_ge(sem.parr, arrivals)
+        V.tensor_reduce(T.FM[:, 0:1], T.C[:, 0:SW * (N + 1):2], AX, mx).then_inc(sem.fm, 1)
+        V.tensor_reduce(T.S[:, 0:1], T.C[:, 1:SW * (N + 1):2], AX, add).then_inc(sem.sready, 1)
+        V.wait_ge(sem.fm, 1)
+        V.tensor_scalar(T.S[:, 1:2], T.FM[:, 0:1], 0.125, None, mul).then_inc(sem.sready, 1)
 
+    g.sync.wait_ge(sem.nready, NG)
+    g.sync.dma_start(T.y[:, LO:HI], T.NS[:, LO:HI]).then_inc(sem.yst, 16)
     if is_hub:
         g.scalar.wait_ge(sem.nbready, 1)
-        g.scalar.dma_start(T.y[:, 0:LO], T.NB[:, rank, 2:4]).then_inc(sem.yst, 16)
-        g.scalar.dma_start(T.y[:, HI:W], T.NB[:, rank + 1, 0:2]).then_inc(sem.yst, 16)
-        g.scalar.wait_ge(sem.nready, 1)
-        g.scalar.dma_start(T.y[:, LO:HI], T.NS[:, LO:HI]).then_inc(sem.yst, 16)
+        g.scalar.dma_start(T.y[:, 0:LO], T.NB[:, rank, 2:4]).then_inc(sem.bst, 16)
+        g.scalar.dma_start(T.y[:, HI:W], T.NB[:, rank + 1, 0:2]).then_inc(sem.bst, 16)
         g.sync.wait_ge(sem.sready, 2)
         g.sync.dma_start(T.s[:], T.S[:]).then_inc(sem.sst, 16)
     else:
-        g.scalar.wait_ge(sem.nready, 1)
-        g.scalar.dma_start(T.y[:, LO:HI], T.NS[:, LO:HI]).then_inc(sem.yst, 16)
         g.scalar.wait_ge(sem.yarr, len(_bits(yb_eng[rank])))
-        g.scalar.dma_start(T.y[:, 0:LO], T.YB[:, 0, 2:4]).then_inc(sem.yst, 16)
-        g.scalar.dma_start(T.y[:, HI:W], T.YB[:, 1, 0:2]).then_inc(sem.yst, 16)
+        g.scalar.dma_start(T.y[:, 0:LO], T.YB[:, 0, 2:4]).then_inc(sem.bst, 16)
+        g.scalar.dma_start(T.y[:, HI:W], T.YB[:, 1, 0:2]).then_inc(sem.bst, 16)
         hub = serve[rank]
         g.sync.wait_ge(sem.farr, len(_bits(mask_to(hub, [k for k in range(N) if serve.get(k) == hub]))))
         g.sync.dma_start(T.s[:], T.SL[:]).then_inc(sem.sst, 16)
-    g.scalar.wait_ge(sem.yst, 48)
+    g.scalar.wait_ge(sem.bst, 32)
+    g.sync.wait_ge(sem.yst, 16)
     g.sync.wait_ge(sem.sst, 16)

@@ -16,7 +16,7 @@ SCRATCH = {
     "pS": ("sbuf", [128, NG, GW + 8], F32),
     "A0": ("psum", [128, 512], F32), "A1": ("psum", [128, 512], F32),
     "A2": ("psum", [128, 512], F32), "A3": ("psum", [128, 512], F32),
-    "mS": ("sbuf", [128, W], F32), "R3": ("sbuf", [128, W], F32), "J": ("sbuf", [128, W], F32),
+    "tS": ("sbuf", [128, W], F32), "R3": ("sbuf", [128, W], F32), "J": ("sbuf", [128, W], F32),
     "NS": ("sbuf", [128, W], F32),
     "C": ("sbuf", [128, SW * (N + 1)], F32),
     "X": ("sbuf", [128, M, 8], F32), "H": ("sbuf", [128, M, 4], F32), "M8": ("sbuf", [128, M, 4], F32),
@@ -28,7 +28,8 @@ SCRATCH = {
     "YB": ("sbuf", [128, 2, 4], F32),
     "SL": ("sbuf", [128, 2], F32),
 }
-SEMAPHORES = ["ul", "bl", "el", "vs", "k0", "k1", "k2", "k3", "pready", "nready", "nbready", "sready",
+SEMAPHORES = ["ul", "bl", "el", "vs", "k0", "k1", "k2", "k3", "t0", "t1", "t2", "t3", "dq",
+              "pready", "nready", "nbready", "sready",
               "xs", "hs", "ps", "es", "ws", "ds", "n8", "cs", "fm",
               "earr", "parr", "yarr", "farr", "lsem", "yst", "bst", "sst"]
 
@@ -75,12 +76,12 @@ def rank_program(g, core, T, topo):
 
     E = T.F[:, rank, :]
     OWN = T.C[:, SW * rank:SW * rank + SW]
-    g.sync.dma_start(T.U[:], T.u[:]).then_inc(sem.ul, 16)
-    g.scalar.dma_start(T.B[:], T.b[:]).then_inc(sem.bl, 16)
     g.sync.dma_start(T.F[:, rank, 0:4], T.u[:, 0:4]).then_inc(sem.el, 16)
     g.scalar.dma_start(T.F[:, rank, 8:10], T.b[:, 0:2]).then_inc(sem.el, 16)
     g.sync.dma_start(T.F[:, rank, 4:8], T.u[:, W - 4:W]).then_inc(sem.el, 16)
     g.scalar.dma_start(T.F[:, rank, 10:12], T.b[:, W - 2:W]).then_inc(sem.el, 16)
+    g.sync.dma_start(T.U[:], T.u[:]).then_inc(sem.ul, 16)
+    g.scalar.dma_start(T.B[:], T.b[:]).then_inc(sem.bl, 16)
 
     sent = 0
     dests = hub_dests(rank)
@@ -119,6 +120,7 @@ def rank_program(g, core, T, topo):
 
     G = range(NG)
     K = [sem["k%d" % q] for q in G]
+    TB = [sem["t%d" % q] for q in G]
     AP = [T["A%d" % q] for q in G]
     lo = [max(LO, q * GW) for q in G]
     hi = [min(HI, (q + 1) * GW) for q in G]
@@ -130,38 +132,43 @@ def rank_program(g, core, T, topo):
         V.memset(T.C[:, SW * N + 3:SW * N + SW:2], 0.0).then_inc(sem.vs, 1)
 
     A.wait_ge(sem.ul, 16)
+    for q in G:
+        A.activation(AP[q][:, 0:wd[q]], T.U[:, lo[q]:hi[q]], Copy, scale=-8.0).then_inc(K[q], 1)
     A.wait_ge(sem.bl, 16)
     for q in G:
-        A.activation(AP[q][:, 0:wd[q]], T.B[:, lo[q]:hi[q]], Copy, scale=4.0).then_inc(K[q], 1)
-        A.activation(T.mS[:, lo[q]:hi[q]], T.U[:, lo[q]:hi[q]], Copy, scale=-8.0).then_inc(K[q], 1)
+        A.activation(T.tS[:, lo[q]:hi[q]], T.B[:, lo[q]:hi[q]], Copy, scale=4.0).then_inc(TB[q], 1)
     V.wait_ge(sem.ul, 16)
     for q in G:
         V.tensor_tensor(T.pS[:, q, 0:wd[q] + 3], T.U[:, lo[q] - 2:hi[q] + 1], T.U[:, lo[q] - 1:hi[q] + 2],
                         add).then_inc(K[q], 1)
     for q in G:
-        V.wait_ge(K[q], 3)
+        V.wait_ge(K[q], 2)
         V.tensor_tensor(AP[q][:, 0:wd[q]], AP[q][:, 0:wd[q]], T.pS[:, q, 0:wd[q]], add).then_inc(K[q], 1)
     for q in G:
-        V.wait_ge(K[q], 4)
+        V.wait_ge(K[q], 3)
         V.tensor_tensor(AP[q][:, 0:wd[q]], AP[q][:, 0:wd[q]], T.pS[:, q, 3:wd[q] + 3], add).then_inc(K[q], 1)
     for q in G:
-        V.wait_ge(K[q], 5)
-        V.tensor_tensor(T.R3[:, lo[q]:hi[q]], AP[q][:, 0:wd[q]], T.mS[:, lo[q]:hi[q]], add).then_inc(K[q], 1)
+        V.wait_ge(K[q], 4)
+        V.wait_ge(TB[q], 1)
+        V.tensor_tensor(T.R3[:, lo[q]:hi[q]], AP[q][:, 0:wd[q]], T.tS[:, lo[q]:hi[q]], add).then_inc(K[q], 1)
     for q in G:
-        V.wait_ge(K[q], 6)
+        V.wait_ge(K[q], 5)
         V.tensor_reduce(T.C[:, own + 2 * q:own + 2 * q + 1], T.R3[:, lo[q]:hi[q]], AX, mx,
                         apply_absolute_value=True).then_inc(sem.pready, 1)
     for q in G:
-        A.wait_ge(K[q], 6)
+        A.wait_ge(K[q], 5)
         A.activation(T.J[:, lo[q]:hi[q]], T.R3[:, lo[q]:hi[q]], Square, scale=1.0 / 384.0,
                      accum_out=T.C[:, own + 2 * q + 1:own + 2 * q + 2]).then_inc(sem.pready, 1)
+    for q in G:
+        A.activation(AP[q][:, 0:wd[q]], T.R3[:, lo[q]:hi[q]], Copy, scale=0.125).then_inc(sem.dq, 1)
 
-    def new_inner():
-        for q in G:
-            A.activation(T.NS[:, lo[q]:hi[q]], AP[q][:, 0:wd[q]], Copy, scale=0.125).then_inc(sem.nready, 1)
+    def new_inner(q):
+        V.tensor_tensor(T.NS[:, lo[q]:hi[q]], AP[q][:, 0:wd[q]], T.U[:, lo[q]:hi[q]], add).then_inc(sem.nready, 1)
 
     if not is_hub:
-        new_inner()
+        V.wait_ge(sem.dq, NG)
+        for q in G:
+            new_inner(q)
     else:
         sl = SW * N
         V.wait_ge(sem.el, 64)
@@ -178,12 +185,16 @@ def rank_program(g, core, T, topo):
         A.activation(T.H[:, N, 2:4], T.F[:, 0, 8:10], Copy, scale=4.0).then_inc(sem.hs, 1)
         A.wait_ge(sem.xs, 4)
         A.activation(T.M8[:], T.X[:, :, 2:6], Copy, scale=-8.0).then_inc(sem.hs, 1)
+        V.wait_ge(sem.dq, NG)
+        new_inner(0)
         V.wait_ge(sem.xs, 4)
         V.tensor_tensor(T.pb[:], T.X[:, :, 0:7], T.X[:, :, 1:8], add).then_inc(sem.ps, 1)
-        V.wait_ge(sem.hs, 5)
-        V.tensor_tensor(T.eb[:], T.H[:], T.M8[:], add).then_inc(sem.es, 1)
+        new_inner(1)
         V.wait_ge(sem.ps, 1)
         V.tensor_tensor(T.vb[:], T.pb[:, :, 0:4], T.pb[:, :, 3:7], add).then_inc(sem.ws, 1)
+        V.wait_ge(sem.hs, 5)
+        V.tensor_tensor(T.eb[:], T.H[:], T.M8[:], add).then_inc(sem.es, 1)
+        new_inner(2)
         V.wait_ge(sem.es, 1)
         V.wait_ge(sem.ws, 1)
         V.tensor_tensor(T.db[:], T.vb[:], T.eb[:], add).then_inc(sem.ds, 1)
@@ -192,12 +203,12 @@ def rank_program(g, core, T, topo):
         for j in range(4):
             V.tensor_reduce(T.C[:, sl + 2 * j:sl + 2 * j + 1], T.db[:, 0:N, j], AX, mx,
                             apply_absolute_value=True).then_inc(sem.cs, 1)
+        new_inner(3)
         A.wait_ge(sem.ds, 1)
         A.activation(T.jb[:, 0:N, :], T.db[:, 0:N, :], Square, scale=1.0 / 384.0,
                      accum_out=T.C[:, sl + 1:sl + 2]).then_inc(sem.cs, 1)
         A.wait_ge(sem.n8, 1)
         A.activation(T.NB[:], T.nb[:], Copy, scale=0.125).then_inc(sem.nbready, 1)
-        new_inner()
         V.wait_ge(sem.vs, 1)
         V.wait_ge(sem.cs, 5)
         V.wait_ge(sem.pready, 2 * NG)

@@ -6,31 +6,35 @@ W = 256
 LO, HI = 2, W - 2
 NG = 4
 GW = W // NG
-M = N + 1
-SW = 2 * NG
+NH = 2
+SW = 2 * NH
+SEAM = 2 * SW
+CW = SEAM + SW * N
+NE = CW // 2
 F32 = "float32"
 
 SCRATCH = {
     "U": ("sbuf", [128, W], F32), "B": ("sbuf", [128, W], F32),
-    "F": ("sbuf", [128, N, 12], F32),
+    "XF": ("sbuf", [128, 2 * N + 2, 6], F32),
     "pS": ("sbuf", [128, NG, GW + 8], F32),
     "A0": ("psum", [128, 512], F32), "A1": ("psum", [128, 512], F32),
     "A2": ("psum", [128, 512], F32), "A3": ("psum", [128, 512], F32),
-    "tS": ("sbuf", [128, W], F32), "R3": ("sbuf", [128, W], F32), "J": ("sbuf", [128, W], F32),
+    "R3": ("sbuf", [128, W], F32), "J": ("sbuf", [128, W], F32),
     "NS": ("sbuf", [128, W], F32),
-    "C": ("sbuf", [128, SW * (N + 1)], F32),
-    "X": ("sbuf", [128, M, 8], F32), "H": ("sbuf", [128, M, 4], F32), "M8": ("sbuf", [128, M, 4], F32),
-    "pb": ("sbuf", [128, M, 7], F32), "vb": ("sbuf", [128, M, 4], F32), "eb": ("sbuf", [128, M, 4], F32),
-    "db": ("sbuf", [128, M, 4], F32), "nb": ("sbuf", [128, M, 4], F32), "NB": ("sbuf", [128, M, 4], F32),
-    "jb": ("sbuf", [128, M, 4], F32),
-    "FM": ("sbuf", [128, 4], F32),
-    "S": ("sbuf", [128, 2], F32),
+    "C": ("sbuf", [128, CW], F32),
+    "ONE": ("sbuf", [128, NE], F32),
+    "Z": ("sbuf", [128, CW], F32),
+    "J2": ("sbuf", [128, NE], F32),
+    "P7": ("sbuf", [128, N, 7], F32), "Hb": ("sbuf", [128, N, 4], F32), "M8": ("sbuf", [128, N, 4], F32),
+    "vb": ("sbuf", [128, N, 4], F32), "eb": ("sbuf", [128, N, 4], F32),
+    "db": ("sbuf", [128, N, 4], F32), "nb": ("sbuf", [128, N, 4], F32), "NB": ("sbuf", [128, N, 4], F32),
+    "jb": ("sbuf", [128, N, 4], F32),
     "YB": ("sbuf", [128, 2, 4], F32),
     "SL": ("sbuf", [128, 2], F32),
 }
-SEMAPHORES = ["ul", "bl", "el", "vs", "k0", "k1", "k2", "k3", "t0", "t1", "t2", "t3", "dq",
+SEMAPHORES = ["ul", "bl", "el", "el2", "vs", "k0", "k1", "k2", "k3", "t0", "t1", "t2", "t3",
               "pready", "nready", "nbready", "sready",
-              "xs", "hs", "ps", "es", "ws", "ds", "n8", "cs", "fm",
+              "hs", "ps", "es", "ws", "ds", "n8", "cs",
               "earr", "parr", "yarr", "farr", "lsem", "yst", "bst", "sst"]
 
 
@@ -74,26 +78,35 @@ def rank_program(g, core, T, topo):
         rid, pid = topo.addr(cores[dst], core)
         return DstId(rid=rid, pnc=pid)
 
-    E = T.F[:, rank, :]
-    OWN = T.C[:, SW * rank:SW * rank + SW]
-    g.sync.dma_start(T.F[:, rank, 0:4], T.u[:, 0:4]).then_inc(sem.el, 16)
-    g.scalar.dma_start(T.F[:, rank, 8:10], T.b[:, 0:2]).then_inc(sem.el, 16)
-    g.sync.dma_start(T.F[:, rank, 4:8], T.u[:, W - 4:W]).then_inc(sem.el, 16)
-    g.scalar.dma_start(T.F[:, rank, 10:12], T.b[:, W - 2:W]).then_inc(sem.el, 16)
+    def slot(k, h):
+        p = (k - h) % N
+        return T.XF[:, 2 * p + 1:2 * p + 3, :]
+
+    E = T.XF[:, 1:3, :]
+    own = SEAM + SW * rank
+    OWN = T.C[:, own:own + SW]
+    g.sync.dma_start(T.XF[:, 1, 2:6], T.u[:, 0:4]).then_inc(sem.el, 16)
+    g.scalar.dma_start(T.XF[:, 1, 0:2], T.b[:, 0:2]).then_inc(sem.el, 16)
+    g.sync.dma_start(T.XF[:, 2, 0:4], T.u[:, W - 4:W]).then_inc(sem.el, 16)
+    g.scalar.dma_start(T.XF[:, 2, 4:6], T.b[:, W - 2:W]).then_inc(sem.el, 16)
     g.sync.dma_start(T.U[:], T.u[:]).then_inc(sem.ul, 16)
     g.scalar.dma_start(T.B[:], T.b[:]).then_inc(sem.bl, 16)
+    if is_hub:
+        g.sync.dma_start(T.XF[:, 2 * N + 1, 2:6], T.u[:, 0:4]).then_inc(sem.el2, 16)
+        g.scalar.dma_start(T.XF[:, 2 * N + 1, 0:2], T.b[:, 0:2]).then_inc(sem.el2, 16)
 
     sent = 0
     dests = hub_dests(rank)
     m_hub = mask_to(rank, dests)
     g.wait_ge(sem.el, 64)
     g.remote_dma_fused([RemoteDMATransfer(dst_ids=[did(h) for h in dests], dma_engine_mask=m_hub, remote_sem=sem.earr,
-                                          srcs=[E], dsts=[E for h in dests])], local_sem=sem.lsem)
+                                          srcs=[E], dsts=[slot(rank, h) for h in dests])], local_sem=sem.lsem)
     sent += len(_bits(m_hub))
-    g.wait_ge(sem.pready, 2 * NG)
+    g.wait_ge(sem.pready, 2 * NH)
     g.remote_dma_fused([RemoteDMATransfer(dst_ids=[did(h) for h in dests], dma_engine_mask=m_hub, remote_sem=sem.parr,
                                           srcs=[OWN], dsts=[OWN for h in dests])], local_sem=sem.lsem)
     sent += len(_bits(m_hub))
+    S = T.Z[:, CW - 2:CW]
     yb_eng = {}
     for h in hubs:
         cl = [k for k in range(N) if serve.get(k) == h]
@@ -106,14 +119,15 @@ def rank_program(g, core, T, topo):
                 yb_eng[k] = sum(bits[i * per:(i + 1) * per])
     if is_hub and clients:
         g.wait_ge(sem.nbready, 1)
+        pos = {k: (k - rank) % N for k in clients}
         g.remote_dma_fused([RemoteDMATransfer(dst_ids=[did(k)], dma_engine_mask=yb_eng[k], remote_sem=sem.yarr,
-                                              srcs=[T.NB[:, k:k + 2, :]], dsts=[T.YB[:]]) for k in clients],
-                           local_sem=sem.lsem)
+                                              srcs=[T.NB[:, pos[k] - 1:pos[k] + 1, :]], dsts=[T.YB[:]])
+                            for k in clients], local_sem=sem.lsem)
         sent += sum(len(_bits(yb_eng[k])) for k in clients)
         m_cl = mask_to(rank, clients)
         g.wait_ge(sem.sready, 2)
         g.remote_dma_fused([RemoteDMATransfer(dst_ids=[did(k) for k in clients], dma_engine_mask=m_cl,
-                                              remote_sem=sem.farr, srcs=[T.S[:]], dsts=[T.SL[:] for k in clients])],
+                                              remote_sem=sem.farr, srcs=[S], dsts=[T.SL[:] for k in clients])],
                            local_sem=sem.lsem)
         sent += len(_bits(m_cl))
     g.wait_ge(sem.lsem, sent)
@@ -125,18 +139,22 @@ def rank_program(g, core, T, topo):
     lo = [max(LO, q * GW) for q in G]
     hi = [min(HI, (q + 1) * GW) for q in G]
     wd = [hi[q] - lo[q] for q in G]
-    own = SW * rank
+    per_h = NG // NH
     arrivals = sum(len(_bits(mask_to(x, hub_dests(x)))) for x in range(N) if x != rank)
 
     if is_hub:
-        V.memset(T.C[:, SW * N + 3:SW * N + SW:2], 0.0).then_inc(sem.vs, 1)
+        V.memset(T.C[:, 3:SEAM:2], 0.0).then_inc(sem.vs, 1)
+        V.memset(T.ONE[:, 0:3], 1.0).then_inc(sem.vs, 1)
+        V.memset(T.ONE[:, 3:4], 0.25).then_inc(sem.vs, 1)
+        V.memset(T.ONE[:, 4:NE - 1], 1.0).then_inc(sem.vs, 1)
+        V.memset(T.ONE[:, NE - 1:NE], 0.5).then_inc(sem.vs, 1)
 
     A.wait_ge(sem.ul, 16)
     for q in G:
         A.activation(AP[q][:, 0:wd[q]], T.U[:, lo[q]:hi[q]], Copy, scale=-8.0).then_inc(K[q], 1)
-    A.wait_ge(sem.bl, 16)
     for q in G:
-        A.activation(T.tS[:, lo[q]:hi[q]], T.B[:, lo[q]:hi[q]], Copy, scale=4.0).then_inc(TB[q], 1)
+        A.wait_ge(K[q], 4)
+        A.activation(AP[q][:, 0:wd[q]], AP[q][:, 0:wd[q]], Copy, scale=0.25).then_inc(K[q], 1)
     V.wait_ge(sem.ul, 16)
     for q in G:
         V.tensor_tensor(T.pS[:, q, 0:wd[q] + 3], T.U[:, lo[q] - 2:hi[q] + 1], T.U[:, lo[q] - 1:hi[q] + 2],
@@ -147,85 +165,78 @@ def rank_program(g, core, T, topo):
     for q in G:
         V.wait_ge(K[q], 3)
         V.tensor_tensor(AP[q][:, 0:wd[q]], AP[q][:, 0:wd[q]], T.pS[:, q, 3:wd[q] + 3], add).then_inc(K[q], 1)
-    for q in G:
-        V.wait_ge(K[q], 4)
-        V.wait_ge(TB[q], 1)
-        V.tensor_tensor(T.R3[:, lo[q]:hi[q]], AP[q][:, 0:wd[q]], T.tS[:, lo[q]:hi[q]], add).then_inc(K[q], 1)
+    V.wait_ge(sem.bl, 16)
     for q in G:
         V.wait_ge(K[q], 5)
-        V.tensor_reduce(T.C[:, own + 2 * q:own + 2 * q + 1], T.R3[:, lo[q]:hi[q]], AX, mx,
+        V.tensor_tensor(T.R3[:, lo[q]:hi[q]], AP[q][:, 0:wd[q]], T.B[:, lo[q]:hi[q]], add).then_inc(K[q], 1)
+    for h in range(NH):
+        a, z = lo[h * per_h], hi[(h + 1) * per_h - 1]
+        for q in range(h * per_h, (h + 1) * per_h):
+            V.wait_ge(K[q], 6)
+        V.tensor_reduce(T.C[:, own + 2 * h:own + 2 * h + 1], T.R3[:, a:z], AX, mx,
                         apply_absolute_value=True).then_inc(sem.pready, 1)
+    for h in range(NH):
+        a, z = lo[h * per_h], hi[(h + 1) * per_h - 1]
+        for q in range(h * per_h, (h + 1) * per_h):
+            A.wait_ge(K[q], 6)
+        A.activation(T.J[:, a:z], T.R3[:, a:z], Square, scale=1.0 / 96.0,
+                     accum_out=T.C[:, own + 2 * h + 1:own + 2 * h + 2]).then_inc(sem.pready, 1)
     for q in G:
-        A.wait_ge(K[q], 5)
-        A.activation(T.J[:, lo[q]:hi[q]], T.R3[:, lo[q]:hi[q]], Square, scale=1.0 / 384.0,
-                     accum_out=T.C[:, own + 2 * q + 1:own + 2 * q + 2]).then_inc(sem.pready, 1)
+        A.activation(AP[q][:, 0:wd[q]], T.R3[:, lo[q]:hi[q]], Copy, scale=0.5).then_inc(TB[q], 1)
     for q in G:
-        A.activation(AP[q][:, 0:wd[q]], T.R3[:, lo[q]:hi[q]], Copy, scale=0.125).then_inc(sem.dq, 1)
-
-    def new_inner(q):
+        V.wait_ge(TB[q], 1)
         V.tensor_tensor(T.NS[:, lo[q]:hi[q]], AP[q][:, 0:wd[q]], T.U[:, lo[q]:hi[q]], add).then_inc(sem.nready, 1)
 
-    if not is_hub:
-        V.wait_ge(sem.dq, NG)
-        for q in G:
-            new_inner(q)
-    else:
-        sl = SW * N
-        V.wait_ge(sem.el, 64)
-        V.wait_ge(sem.earr, arrivals)
-        V.tensor_copy(T.X[:, 1:M, 0:4], T.F[:, 0:N, 4:8]).then_inc(sem.xs, 1)
-        V.tensor_copy(T.X[:, 0:N, 4:8], T.F[:, 0:N, 0:4]).then_inc(sem.xs, 1)
-        V.tensor_copy(T.X[:, 0, 0:4], T.F[:, N - 1, 4:8]).then_inc(sem.xs, 1)
-        V.tensor_copy(T.X[:, N, 4:8], T.F[:, 0, 0:4]).then_inc(sem.xs, 1)
-        A.wait_ge(sem.el, 64)
-        A.wait_ge(sem.earr, arrivals)
-        A.activation(T.H[:, 1:M, 0:2], T.F[:, 0:N, 10:12], Copy, scale=4.0).then_inc(sem.hs, 1)
-        A.activation(T.H[:, 0:N, 2:4], T.F[:, 0:N, 8:10], Copy, scale=4.0).then_inc(sem.hs, 1)
-        A.activation(T.H[:, 0, 0:2], T.F[:, N - 1, 10:12], Copy, scale=4.0).then_inc(sem.hs, 1)
-        A.activation(T.H[:, N, 2:4], T.F[:, 0, 8:10], Copy, scale=4.0).then_inc(sem.hs, 1)
-        A.wait_ge(sem.xs, 4)
-        A.activation(T.M8[:], T.X[:, :, 2:6], Copy, scale=-8.0).then_inc(sem.hs, 1)
-        V.wait_ge(sem.dq, NG)
-        new_inner(0)
-        V.wait_ge(sem.xs, 4)
-        V.tensor_tensor(T.pb[:], T.X[:, :, 0:7], T.X[:, :, 1:8], add).then_inc(sem.ps, 1)
-        new_inner(1)
-        V.wait_ge(sem.ps, 1)
-        V.tensor_tensor(T.vb[:], T.pb[:, :, 0:4], T.pb[:, :, 3:7], add).then_inc(sem.ws, 1)
-        V.wait_ge(sem.hs, 5)
-        V.tensor_tensor(T.eb[:], T.H[:], T.M8[:], add).then_inc(sem.es, 1)
-        new_inner(2)
+    if is_hub:
+        def Lh(a, z):
+            return T.XF[:, 2:2 * N + 2:2, a:z]
+
+        def Rh(a, z):
+            return T.XF[:, 3:2 * N + 2:2, a:z]
+
+        for Q in (V, A):
+            Q.wait_ge(sem.el, 64)
+            Q.wait_ge(sem.el2, 32)
+            Q.wait_ge(sem.earr, arrivals)
+        V.tensor_tensor(T.P7[:, :, 0:3], Lh(0, 3), Lh(1, 4), add).then_inc(sem.ps, 1)
+        V.tensor_tensor(T.P7[:, :, 4:7], Rh(2, 5), Rh(3, 6), add).then_inc(sem.ps, 1)
+        V.tensor_tensor(T.P7[:, :, 3:4], Lh(3, 4), Rh(2, 3), add).then_inc(sem.ps, 1)
+        A.activation(T.Hb[:, :, 0:2], Lh(4, 6), Copy, scale=4.0).then_inc(sem.hs, 1)
+        A.activation(T.Hb[:, :, 2:4], Rh(0, 2), Copy, scale=4.0).then_inc(sem.hs, 1)
+        A.activation(T.M8[:, :, 0:2], Lh(2, 4), Copy, scale=-8.0).then_inc(sem.hs, 1)
+        A.activation(T.M8[:, :, 2:4], Rh(2, 4), Copy, scale=-8.0).then_inc(sem.hs, 1)
+        V.wait_ge(sem.hs, 4)
+        V.tensor_tensor(T.eb[:], T.Hb[:], T.M8[:], add).then_inc(sem.es, 1)
+        V.wait_ge(sem.ps, 3)
+        V.tensor_tensor(T.vb[:], T.P7[:, :, 0:4], T.P7[:, :, 3:7], add).then_inc(sem.ws, 1)
         V.wait_ge(sem.es, 1)
         V.wait_ge(sem.ws, 1)
         V.tensor_tensor(T.db[:], T.vb[:], T.eb[:], add).then_inc(sem.ds, 1)
-        V.tensor_tensor(T.nb[:], T.vb[:], T.H[:], add).then_inc(sem.n8, 1)
+        V.tensor_tensor(T.nb[:], T.vb[:], T.Hb[:], add).then_inc(sem.n8, 1)
         V.wait_ge(sem.ds, 1)
         for j in range(4):
-            V.tensor_reduce(T.C[:, sl + 2 * j:sl + 2 * j + 1], T.db[:, 0:N, j], AX, mx,
+            V.tensor_reduce(T.C[:, 2 * j:2 * j + 1], T.db[:, :, j], AX, mx,
                             apply_absolute_value=True).then_inc(sem.cs, 1)
-        new_inner(3)
         A.wait_ge(sem.ds, 1)
-        A.activation(T.jb[:, 0:N, :], T.db[:, 0:N, :], Square, scale=1.0 / 384.0,
-                     accum_out=T.C[:, sl + 1:sl + 2]).then_inc(sem.cs, 1)
+        A.activation(T.jb[:], T.db[:], Square, scale=1.0 / 384.0, accum_out=T.C[:, 1:2]).then_inc(sem.cs, 1)
         A.wait_ge(sem.n8, 1)
         A.activation(T.NB[:], T.nb[:], Copy, scale=0.125).then_inc(sem.nbready, 1)
-        V.wait_ge(sem.vs, 1)
-        V.wait_ge(sem.cs, 5)
-        V.wait_ge(sem.pready, 2 * NG)
-        V.wait_ge(sem.parr, arrivals)
-        V.tensor_reduce(T.FM[:, 0:1], T.C[:, 0:SW * (N + 1):2], AX, mx).then_inc(sem.fm, 1)
-        V.tensor_reduce(T.S[:, 0:1], T.C[:, 1:SW * (N + 1):2], AX, add).then_inc(sem.sready, 1)
-        V.wait_ge(sem.fm, 1)
-        V.tensor_scalar(T.S[:, 1:2], T.FM[:, 0:1], 0.125, None, mul).then_inc(sem.sready, 1)
+        for Q in (V, A):
+            Q.wait_ge(sem.vs, 5)
+            Q.wait_ge(sem.cs, 5)
+            Q.wait_ge(sem.pready, 2 * NH)
+            Q.wait_ge(sem.parr, arrivals)
+        V.tensor_tensor_scan(T.Z[:, 1:CW:2], T.C[:, 0:CW:2], T.ONE[:], 0.0, mx, mul).then_inc(sem.sready, 1)
+        A.activation(T.J2[:], T.C[:, 1:CW:2], Copy, accum_out=T.Z[:, CW - 2:CW - 1]).then_inc(sem.sready, 1)
 
     g.sync.wait_ge(sem.nready, NG)
     g.sync.dma_start(T.y[:, LO:HI], T.NS[:, LO:HI]).then_inc(sem.yst, 16)
     if is_hub:
         g.scalar.wait_ge(sem.nbready, 1)
-        g.scalar.dma_start(T.y[:, 0:LO], T.NB[:, rank, 2:4]).then_inc(sem.bst, 16)
-        g.scalar.dma_start(T.y[:, HI:W], T.NB[:, rank + 1, 0:2]).then_inc(sem.bst, 16)
+        g.scalar.dma_start(T.y[:, 0:LO], T.NB[:, N - 1, 2:4]).then_inc(sem.bst, 16)
+        g.scalar.dma_start(T.y[:, HI:W], T.NB[:, 0, 0:2]).then_inc(sem.bst, 16)
         g.sync.wait_ge(sem.sready, 2)
-        g.sync.dma_start(T.s[:], T.S[:]).then_inc(sem.sst, 16)
+        g.sync.dma_start(T.s[:], S).then_inc(sem.sst, 16)
     else:
         g.scalar.wait_ge(sem.yarr, len(_bits(yb_eng[rank])))
         g.scalar.dma_start(T.y[:, 0:LO], T.YB[:, 0, 2:4]).then_inc(sem.bst, 16)

from concourse.bass import DstId, RemoteDMATransfer
from concourse.mybir import AluOpType, AxisListType, ActivationFunctionType

N = 9
W = 256
LO, HI = 2, W - 2
NG = 4
GW = W // NG
NH = 2
SW = 2 * NH
SEAM = 2 * SW
CW = SEAM + SW * N
NE = CW // 2
F32 = "float32"

SCRATCH = {
    "U": ("sbuf", [128, W], F32), "B": ("sbuf", [128, W], F32),
    "XF": ("sbuf", [128, 2 * N + 2, 6], F32),
    "pS": ("sbuf", [128, NG, GW + 8], F32),
    "A0": ("psum", [128, 512], F32), "A1": ("psum", [128, 512], F32),
    "A2": ("psum", [128, 512], F32), "A3": ("psum", [128, 512], F32),
    "R3": ("sbuf", [128, W], F32), "J": ("sbuf", [128, W], F32),
    "NS": ("sbuf", [128, W], F32),
    "C": ("sbuf", [128, CW], F32),
    "ONE": ("sbuf", [128, NE], F32),
    "Z": ("sbuf", [128, CW], F32),
    "J2": ("sbuf", [128, NE], F32),
    "P7": ("sbuf", [128, N, 7], F32), "Hb": ("sbuf", [128, N, 4], F32), "M8": ("sbuf", [128, N, 4], F32),
    "vb": ("sbuf", [128, N, 4], F32), "eb": ("sbuf", [128, N, 4], F32),
    "db": ("sbuf", [128, N, 4], F32), "nb": ("sbuf", [128, N, 4], F32), "NB": ("sbuf", [128, N, 4], F32),
    "jb": ("sbuf", [128, N, 4], F32),
    "YB": ("sbuf", [128, 2, 4], F32),
    "SL": ("sbuf", [128, 2], F32),
}
SEMAPHORES = ["ul", "bl", "el", "el2", "vs", "k0", "k1", "k2", "k3", "t0", "t1", "t2", "t3",
              "pready", "nready", "nbready", "sready",
              "hs", "ps", "es", "ws", "ds", "n8", "cs",
              "earr", "parr", "yarr", "farr", "lsem", "yst", "bst", "sst"]


def _bits(m):
    return [1 << i for i in range(16) if (m >> i) & 1]


def rank_program(g, core, T, topo):
    rank = T.rank_of(core)
    if rank is None:
        return
    cores = list(T.cores)
    sem = T.sem
    V = g.vector
    A = g.scalar
    add, mul, mx = AluOpType.add, AluOpType.mult, AluOpType.max
    AX = AxisListType.X
    Copy, Square = ActivationFunctionType.Copy, ActivationFunctionType.Square

    def both(a, b):
        return topo.may_write(cores[a], cores[b]) and topo.may_write(cores[b], cores[a])

    hubs = [r for r in range(N) if all(both(r, x) for x in range(N) if x != r)]
    serve = {}
    for i, k in enumerate([r for r in range(N) if r not in hubs]):
        same = [h for h in hubs if topo.chip(cores[h]) == topo.chip(cores[k])]
        serve[k] = same[0] if same else hubs[i % len(hubs)]
    is_hub = rank in hubs
    clients = [k for k in range(N) if serve.get(k) == rank]

    def hub_dests(x):
        return [h for h in hubs if h != x]

    def mask_to(x, dests):
        m = topo.mask(cores[x], cores[dests[0]])
        for d_ in dests[1:]:
            m &= topo.mask(cores[x], cores[d_])
        return m

    def did(dst):
        rid, pid = topo.addr(cores[dst], core)
        return DstId(rid=rid, pnc=pid)

    def slot(k, h):
        p = (k - h) % N
        return T.XF[:, 2 * p + 1:2 * p + 3, :]

    E = T.XF[:, 1:3, :]
    own = SEAM + SW * rank
    OWN = T.C[:, own:own + SW]
    g.sync.dma_start(T.XF[:, 1, 2:6], T.u[:, 0:4]).then_inc(sem.el, 16)
    g.scalar.dma_start(T.XF[:, 1, 0:2], T.b[:, 0:2]).then_inc(sem.el, 16)
    g.sync.dma_start(T.XF[:, 2, 0:4], T.u[:, W - 4:W]).then_inc(sem.el, 16)
    g.scalar.dma_start(T.XF[:, 2, 4:6], T.b[:, W - 2:W]).then_inc(sem.el, 16)
    g.sync.dma_start(T.U[:], T.u[:]).then_inc(sem.ul, 16)
    g.scalar.dma_start(T.B[:], T.b[:]).then_inc(sem.bl, 16)
    if is_hub:
        g.sync.dma_start(T.XF[:, 2 * N + 1, 2:6], T.u[:, 0:4]).then_inc(sem.el2, 16)
        g.scalar.dma_start(T.XF[:, 2 * N + 1, 0:2], T.b[:, 0:2]).then_inc(sem.el2, 16)

    sent = 0
    dests = hub_dests(rank)
    m_hub = mask_to(rank, dests)
    g.wait_ge(sem.el, 64)
    g.remote_dma_fused([RemoteDMATransfer(dst_ids=[did(h) for h in dests], dma_engine_mask=m_hub, remote_sem=sem.earr,
                                          srcs=[E], dsts=[slot(rank, h) for h in dests])], local_sem=sem.lsem)
    sent += len(_bits(m_hub))
    g.wait_ge(sem.pready, 2 * NH)
    g.remote_dma_fused([RemoteDMATransfer(dst_ids=[did(h) for h in dests], dma_engine_mask=m_hub, remote_sem=sem.parr,
                                          srcs=[OWN], dsts=[OWN for h in dests])], local_sem=sem.lsem)
    sent += len(_bits(m_hub))
    S = T.Z[:, CW - 2:CW]
    yb_eng = {}
    for h in hubs:
        cl = [k for k in range(N) if serve.get(k) == h]
        if cl:
            bits = _bits(mask_to(h, cl))
            per = 1
            while per * 2 * len(cl) <= len(bits):
                per *= 2
            for i, k in enumerate(cl):
                yb_eng[k] = sum(bits[i * per:(i + 1) * per])
    if is_hub and clients:
        g.wait_ge(sem.nbready, 1)
        pos = {k: (k - rank) % N for k in clients}
        g.remote_dma_fused([RemoteDMATransfer(dst_ids=[did(k)], dma_engine_mask=yb_eng[k], remote_sem=sem.yarr,
                                              srcs=[T.NB[:, pos[k] - 1:pos[k] + 1, :]], dsts=[T.YB[:]])
                            for k in clients], local_sem=sem.lsem)
        sent += sum(len(_bits(yb_eng[k])) for k in clients)
        m_cl = mask_to(rank, clients)
        g.wait_ge(sem.sready, 2)
        g.remote_dma_fused([RemoteDMATransfer(dst_ids=[did(k) for k in clients], dma_engine_mask=m_cl,
                                              remote_sem=sem.farr, srcs=[S], dsts=[T.SL[:] for k in clients])],
                           local_sem=sem.lsem)
        sent += len(_bits(m_cl))
    g.wait_ge(sem.lsem, sent)

    G = range(NG)
    K = [sem["k%d" % q] for q in G]
    TB = [sem["t%d" % q] for q in G]
    AP = [T["A%d" % q] for q in G]
    lo = [max(LO, q * GW) for q in G]
    hi = [min(HI, (q + 1) * GW) for q in G]
    wd = [hi[q] - lo[q] for q in G]
    per_h = NG // NH
    arrivals = sum(len(_bits(mask_to(x, hub_dests(x)))) for x in range(N) if x != rank)

    if is_hub:
        V.memset(T.C[:, 3:SEAM:2], 0.0).then_inc(sem.vs, 1)
        V.memset(T.ONE[:, 0:3], 1.0).then_inc(sem.vs, 1)
        V.memset(T.ONE[:, 3:4], 0.25).then_inc(sem.vs, 1)
        V.memset(T.ONE[:, 4:NE - 1], 1.0).then_inc(sem.vs, 1)
        V.memset(T.ONE[:, NE - 1:NE], 0.5).then_inc(sem.vs, 1)

    A.wait_ge(sem.ul, 16)
    for q in G:
        A.activation(AP[q][:, 0:wd[q]], T.U[:, lo[q]:hi[q]], Copy, scale=-8.0).then_inc(K[q], 1)
    for q in G:
        A.wait_ge(K[q], 4)
        A.activation(AP[q][:, 0:wd[q]], AP[q][:, 0:wd[q]], Copy, scale=0.25).then_inc(K[q], 1)
    V.wait_ge(sem.ul, 16)
    for q in G:
        V.tensor_tensor(T.pS[:, q, 0:wd[q] + 3], T.U[:, lo[q] - 2:hi[q] + 1], T.U[:, lo[q] - 1:hi[q] + 2],
                        add).then_inc(K[q], 1)
    for q in G:
        V.wait_ge(K[q], 2)
        V.tensor_tensor(AP[q][:, 0:wd[q]], AP[q][:, 0:wd[q]], T.pS[:, q, 0:wd[q]], add).then_inc(K[q], 1)
    for q in G:
        V.wait_ge(K[q], 3)
        V.tensor_tensor(AP[q][:, 0:wd[q]], AP[q][:, 0:wd[q]], T.pS[:, q, 3:wd[q] + 3], add).then_inc(K[q], 1)
    V.wait_ge(sem.bl, 16)
    for q in G:
        V.wait_ge(K[q], 5)
        V.tensor_tensor(T.R3[:, lo[q]:hi[q]], AP[q][:, 0:wd[q]], T.B[:, lo[q]:hi[q]], add).then_inc(K[q], 1)
    for h in range(NH):
        a, z = lo[h * per_h], hi[(h + 1) * per_h - 1]
        for q in range(h * per_h, (h + 1) * per_h):
            V.wait_ge(K[q], 6)
        V.tensor_reduce(T.C[:, own + 2 * h:own + 2 * h + 1], T.R3[:, a:z], AX, mx,
                        apply_absolute_value=True).then_inc(sem.pready, 1)
    for h in range(NH):
        a, z = lo[h * per_h], hi[(h + 1) * per_h - 1]
        for q in range(h * per_h, (h + 1) * per_h):
            A.wait_ge(K[q], 6)
        A.activation(T.J[:, a:z], T.R3[:, a:z], Square, scale=1.0 / 96.0,
                     accum_out=T.C[:, own + 2 * h + 1:own + 2 * h + 2]).then_inc(sem.pready, 1)
    for q in G:
        A.activation(AP[q][:, 0:wd[q]], T.R3[:, lo[q]:hi[q]], Copy, scale=0.5).then_inc(TB[q], 1)
    for q in G:
        V.wait_ge(TB[q], 1)
        V.tensor_tensor(T.NS[:, lo[q]:hi[q]], AP[q][:, 0:wd[q]], T.U[:, lo[q]:hi[q]], add).then_inc(sem.nready, 1)

    if is_hub:
        def Lh(a, z):
            return T.XF[:, 2:2 * N + 2:2, a:z]

        def Rh(a, z):
            return T.XF[:, 3:2 * N + 2:2, a:z]

        for Q in (V, A):
            Q.wait_ge(sem.el, 64)
            Q.wait_ge(sem.el2, 32)
            Q.wait_ge(sem.earr, arrivals)
        V.tensor_tensor(T.P7[:, :, 0:3], Lh(0, 3), Lh(1, 4), add).then_inc(sem.ps, 1)
        V.tensor_tensor(T.P7[:, :, 4:7], Rh(2, 5), Rh(3, 6), add).then_inc(sem.ps, 1)
        V.tensor_tensor(T.P7[:, :, 3:4], Lh(3, 4), Rh(2, 3), add).then_inc(sem.ps, 1)
        A.activation(T.Hb[:, :, 0:2], Lh(4, 6), Copy, scale=4.0).then_inc(sem.hs, 1)
        A.activation(T.Hb[:, :, 2:4], Rh(0, 2), Copy, scale=4.0).then_inc(sem.hs, 1)
        A.activation(T.M8[:, :, 0:2], Lh(2, 4), Copy, scale=-8.0).then_inc(sem.hs, 1)
        A.activation(T.M8[:, :, 2:4], Rh(2, 4), Copy, scale=-8.0).then_inc(sem.hs, 1)
        V.wait_ge(sem.hs, 4)
        V.tensor_tensor(T.eb[:], T.Hb[:], T.M8[:], add).then_inc(sem.es, 1)
        V.wait_ge(sem.ps, 3)
        V.tensor_tensor(T.vb[:], T.P7[:, :, 0:4], T.P7[:, :, 3:7], add).then_inc(sem.ws, 1)
        V.wait_ge(sem.es, 1)
        V.wait_ge(sem.ws, 1)
        V.tensor_tensor(T.db[:], T.vb[:], T.eb[:], add).then_inc(sem.ds, 1)
        V.tensor_tensor(T.nb[:], T.vb[:], T.Hb[:], add).then_inc(sem.n8, 1)
        V.wait_ge(sem.ds, 1)
        for j in range(4):
            V.tensor_reduce(T.C[:, 2 * j:2 * j + 1], T.db[:, :, j], AX, mx,
                            apply_absolute_value=True).then_inc(sem.cs, 1)
        A.wait_ge(sem.ds, 1)
        A.activation(T.jb[:], T.db[:], Square, scale=1.0 / 384.0, accum_out=T.C[:, 1:2]).then_inc(sem.cs, 1)
        A.wait_ge(sem.n8, 1)
        A.activation(T.NB[:], T.nb[:], Copy, scale=0.125).then_inc(sem.nbready, 1)
        for Q in (V, A):
            Q.wait_ge(sem.vs, 5)
            Q.wait_ge(sem.cs, 5)
            Q.wait_ge(sem.pready, 2 * NH)
            Q.wait_ge(sem.parr, arrivals)
        V.tensor_tensor_scan(T.Z[:, 1:CW:2], T.C[:, 0:CW:2], T.ONE[:], 0.0, mx, mul).then_inc(sem.sready, 1)
        A.activation(T.J2[:], T.C[:, 1:CW:2], Copy, accum_out=T.Z[:, CW - 2:CW - 1]).then_inc(sem.sready, 1)

    g.sync.wait_ge(sem.nready, NG)
    g.sync.dma_start(T.y[:, LO:HI], T.NS[:, LO:HI]).then_inc(sem.yst, 16)
    if is_hub:
        g.scalar.wait_ge(sem.nbready, 1)
        g.scalar.dma_start(T.y[:, 0:LO], T.NB[:, N - 1, 2:4]).then_inc(sem.bst, 16)
        g.scalar.dma_start(T.y[:, HI:W], T.NB[:, 0, 0:2]).then_inc(sem.bst, 16)
        g.sync.wait_ge(sem.sready, 2)
        g.sync.dma_start(T.s[:], S).then_inc(sem.sst, 16)
    else:
        g.scalar.wait_ge(sem.yarr, len(_bits(yb_eng[rank])))
        g.scalar.dma_start(T.y[:, 0:LO], T.YB[:, 0, 2:4]).then_inc(sem.bst, 16)
        g.scalar.dma_start(T.y[:, HI:W], T.YB[:, 1, 0:2]).then_inc(sem.bst, 16)
        hub = serve[rank]
        g.sync.wait_ge(sem.farr, len(_bits(mask_to(hub, [k for k in range(N) if serve.get(k) == hub]))))
        g.sync.dma_start(T.s[:], T.SL[:]).then_inc(sem.sst, 16)
    g.scalar.wait_ge(sem.bst, 32)
    g.sync.wait_ge(sem.yst, 16)
    g.sync.wait_ge(sem.sst, 16)
